import numpy as np
import ml_dtypes


def mxq(x, axis, fmt="e4m3"):
    dtype, down = {"e4m3": (ml_dtypes.float8_e4m3fn, 7), "e5m2": (ml_dtypes.float8_e5m2, 14)}[fmt]
    v = np.moveaxis(np.asarray(x, np.float32).astype(ml_dtypes.bfloat16).astype(np.float64), axis, -1)
    blocks = v.reshape(v.shape[:-1] + (-1, 32))
    amax = np.abs(blocks).max(-1, keepdims=True)
    byte = np.maximum(np.where(amax > 0, np.frexp(amax)[1] - 1 + 127, 0) - down, 1)
    scale = np.exp2(byte - 127.0)
    codes = (blocks / scale).astype(np.float32).astype(dtype).astype(np.float64)
    return np.moveaxis((codes * scale).reshape(v.shape), -1, axis)


WIDE = False


def mx_kscale(k):
    if not WIDE:
        return np.ones(k)
    levels = np.array([10, -10, 5, -5, 0])
    if k % 512:
        return np.exp2(np.random.permutation(np.resize(levels, k // 32))).repeat(32)
    a = np.empty((k // 512, 16))
    for p in range(k // 512):
        a[p, :8] = np.random.permutation(np.resize(levels, 8))
        for g in range(8):
            far = levels[np.abs(levels - a[p, g]) >= 10]
            a[p, g + 8] = far[np.random.randint(len(far))]
    return np.exp2(a.ravel()).repeat(32)


def f64(x):
    return np.asarray(x).astype(np.float64)


def striped(idx):
    return np.tile(idx.reshape(-1, 16).T, (8, 1)).astype(np.uint16)


def unstriped(offs):
    return offs[:16].T.reshape(-1).astype(np.int64)


E2M1 = np.array([0.0, 0.5, 1.0, 1.5, 2.0, 3.0, 4.0, 6.0, -0.0, -0.5, -1.0, -1.5, -2.0, -3.0, -4.0, -6.0])


def pack_weight(w, fmt):
    k, n = w.shape
    w = f64(np.asarray(w, np.float32).astype(ml_dtypes.bfloat16)).reshape(k // 32, 32, n)
    amax = np.abs(w).max(1)
    if fmt == "e4m3":
        byte = np.frexp(amax)[1] - 1 + 127 - 7
    else:
        mant, ex = np.frexp(amax / 6.0)
        byte = np.where(mant > 0.5, ex, ex - 1) + 127
    byte = np.clip(np.where(amax > 0, byte, 1), 1, 254)
    scaled = (w * np.exp2(127.0 - byte)[:, None, :]).reshape(k, n).astype(np.float32)
    by_word = np.ascontiguousarray(scaled.reshape(k // 512, 128, 4, n).transpose(0, 1, 3, 2))
    if fmt == "e4m3":
        words = by_word.astype(ml_dtypes.float8_e4m3fn).view(np.uint8)
    else:
        c = by_word.astype(ml_dtypes.float4_e2m1fn).view(np.uint8) & 0xF
        words = (c[..., 0::2] | (c[..., 1::2] << 4)).reshape(k // 512, 128, 2 * n)
    return np.ascontiguousarray(words), np.ascontiguousarray(byte.astype(np.uint8).reshape(k // 512, 16, n))


def unpack_weight(words, scales, fmt):
    g, _, n = scales.shape
    words = np.ascontiguousarray(words).reshape(g, 128, n, -1)
    if fmt == "e4m3":
        vals = words.view(ml_dtypes.float8_e4m3fn).astype(np.float64)
    else:
        nib = np.empty((g, 128, n, 4), np.uint8)
        nib[..., 0::2] = words & 0xF
        nib[..., 1::2] = words >> 4
        vals = E2M1[nib]
    vals = vals * np.repeat(np.exp2(scales.astype(np.float64) - 127.0), 8, axis=1)[..., None]
    return vals.transpose(0, 1, 3, 2).reshape(g * 512, n)


def gelu(v):
    return 0.5 * v * (1.0 + np.tanh(np.sqrt(2.0 / np.pi) * (v + 0.044715 * v**3)))


K, T, S, P, H = 1024, 4096, 1024, 512, 512

def setup_inputs():
    n = np.random.standard_normal
    s = mx_kscale(K)[:, None]
    u = mx_kscale(H)[:, None]
    tab_words, tab_scales = pack_weight(n((K, T)) * s, "e4m3")
    w1_words, w1_scales = pack_weight(1.2 * n((K, H)) / np.sqrt(K) / s, "e2m1")
    w2 = 1.6 * n((H, H)) / np.sqrt(H) / u
    w3 = 0.55 * n((K, H)) / np.sqrt(K) / s
    gain = np.exp(0.3 * n(H)) * u[:, 0]
    skip = np.exp(0.3 * n(H)) / u[:, 0]
    return {
        "tab_words": tab_words, "tab_scales": tab_scales,
        "offs": striped(np.random.permutation(T)[:S]),
        "w1_words": w1_words, "w1_scales": w1_scales,
        "gain": gain.astype(np.float32),
        "pos1": striped(np.random.permutation(S)[:P]),
        "w2": w2.astype(np.float32),
        "w3": w3.astype(np.float32),
        "skip": skip.astype(np.float32),
        "wgo": np.exp(0.3 * n((128, P))).astype(np.float32),
    }

def reference(tab_words, tab_scales, offs, w1_words, w1_scales, gain, pos1, w2, w3, skip, wgo):
    v = unpack_weight(tab_words, tab_scales, "e4m3")[:, unstriped(offs)]
    w1 = unpack_weight(w1_words, w1_scales, "e2m1")
    h = f64(gain)[:, None] * np.tanh(w1.T @ v)
    phase = mxq(f64(w3), 0, "e4m3").T @ v
    x = mxq(h[:, unstriped(pos1)], 0, "e4m3")
    stage = mxq(f64(w2), 0, "e4m3").T @ x
    y = np.tanh(stage) + np.cos(phase[:, unstriped(pos1)])
    out = f64(skip)[:, None] * h
    out[:, unstriped(pos1)] = np.tile(f64(wgo), (H // 128, 1)) * y
    return out

@@ -1,0 +1,324 @@
+import math
+from contextlib import ExitStack
+
+import concourse.mybir as mybir
+from concourse.masks import make_identity
+
+K, T, S, PICK, H = 1024, 4096, 1024, 512, 512
+FLOPS = 2 * K * H * S * 2 + 2 * H * H * PICK
+
+F32 = mybir.dt.float32
+BF16 = mybir.dt.bfloat16
+I32 = mybir.dt.int32
+U32 = mybir.dt.uint32
+U16 = mybir.dt.uint16
+U8 = mybir.dt.uint8
+FP8X4 = mybir.dt.float8_e4m3fn_x4
+FP4X4 = mybir.dt.float4_e2m1fn_x4
+ACT = mybir.ActivationFunctionType
+ALU = mybir.AluOpType
+
+P = 128
+PACK = 4
+PASSES = K // (P * PACK)
+BANK = 512
+HALVES = S // BANK
+QUADS = 4
+BLOCKS = PICK // P
+
+
+def tile_list_echo_frame_rework_kernel(
+    tc, tab_words, tab_scales, offs, w1_words, w1_scales, gain, pos1, w2, w3, skip, wgo, out
+):
+    nc = tc.nc
+    with ExitStack() as ctx:
+        keep = ctx.enter_context(tc.tile_pool(name="keep", bufs=1))
+        ring = ctx.enter_context(tc.tile_pool(name="ring", bufs=2))
+        reuse = ctx.enter_context(tc.tile_pool(name="reuse", bufs=1))
+        psum = ctx.enter_context(tc.psum_pool(name="psum", bufs=8))
+
+        def held(shape, dtype, name):
+            return keep.tile(shape, dtype, name=name, align_bytes=64)
+
+        def placed(shape, dtype, name, kib):
+            return reuse.tile(shape, dtype, name=name, align_bytes=64, offset=kib * 1024)
+
+        def bank():
+            return psum.tile([P, BANK], F32, name="bank")
+
+        idx = keep.tile([P, S // 16], U16, name="idx")
+        pick = keep.tile([P, PICK // 16], U16, name="pick")
+        tab = [placed([P, T], U32, f"tab{a}", 16 * a) for a in range(PASSES)]
+        tab_sc = held([P, T], U8, "tab_sc")
+        w1_raw = held([P, PASSES * 2 * H], U8, "w1_raw")
+        w1_sc_raw = held([P, PASSES * H], U8, "w1_sc_raw")
+        v_sc = held([P, PASSES * S], U8, "v_sc")
+        gain_pt = held([P, PACK], F32, "gain_pt")
+        skip_pt = held([P, PACK], F32, "skip_pt")
+        ident = held([P, P], F32, "ident")
+
+        nc.gpsimd.memset(w1_sc_raw[:].bitcast(I32), 0)
+        nc.vector.memset(tab_sc[32:64, :].bitcast(I32), 0)
+        nc.vector.memset(tab_sc[64:128, :].bitcast(I32), 0)
+        nc.vector.memset(v_sc[:].bitcast(I32), 0)
+
+        def load_table(a):
+            words = tab_words[a].rearrange("p t i -> p (t i)")
+            nc.sync.dma_start(tab[a][:].bitcast(I32), words.bitcast(I32))
+
+        nc.sync.dma_start(idx[:], offs)
+        nc.sync.dma_start(tab_sc[0:32, :].bitcast(I32), tab_scales.rearrange("a q t -> (a q) t").bitcast(I32))
+        load_table(0)
+        load_table(1)
+        nc.scalar.dma_start(
+            w1_raw[:].bitcast(I32).rearrange("p (a c) -> p a c", a=PASSES),
+            w1_words.bitcast(I32).rearrange("a p c -> p a c"),
+        )
+        for q in range(QUADS):
+            nc.gpsimd.dma_start(
+                w1_sc_raw[32 * q : 32 * q + 4, :].bitcast(I32).rearrange("r (a c) -> r a c", a=PASSES),
+                w1_scales[:, 4 * q : 4 * q + 4, :].bitcast(I32).rearrange("a r c -> r a c"),
+            )
+        nc.gpsimd.dma_start(gain_pt[:], gain.rearrange("(p t) -> p t", t=PACK))
+        nc.gpsimd.dma_start(skip_pt[:], skip.rearrange("(p t) -> p t", t=PACK))
+        nc.sync.dma_start(pick[:], pos1)
+        make_identity(nc, ident[:])
+
+        v_sc_rows = held([P, S], U8, "v_sc_rows")
+        nc.vector.tensor_copy(v_sc_rows[:], tab_sc[:].indirect(idx[:]))
+        for a in range(PASSES):
+            for q in range(QUADS):
+                row = 16 * a + 4 * q
+                nc.scalar.dma_start(
+                    v_sc[32 * q : 32 * q + 4, a * S : (a + 1) * S].bitcast(I32),
+                    v_sc_rows[row : row + 4, :].bitcast(I32),
+                )
+
+        def load_rows(dst, rows):
+            nc.sync.dma_start(dst, rows.rearrange("(p j) n -> p (j n)", j=PACK))
+
+        w3_first = placed([P, PACK * H], F32, "w3_first", 36)
+        load_rows(w3_first[:], w3[0 : P * PACK, :])
+
+        v0 = placed([P, S], U32, "v0", 32)
+        v1 = held([P, S], U32, "v1")
+        v = [[tile[:, c * BANK : (c + 1) * BANK] for c in range(HALVES)] for tile in (v0, v1)]
+
+        def gather_words(a):
+            for c in range(HALVES):
+                offsets = idx[:, c * BANK // 16 : (c + 1) * BANK // 16]
+                nc.vector.tensor_copy(v[a][c], tab[a][:].indirect(offsets))
+
+        gather_words(0)
+        w3_raw = [w3_first, placed([P, PACK * H], F32, "w3_second", 0)]
+        w2_raw = placed([P, PACK * H], F32, "w2_raw", 8)
+        load_rows(w3_raw[1][:], w3[P * PACK :, :])
+        load_rows(w2_raw[:], w2)
+
+        w1_codes = held([P, PASSES * 2 * H], U8, "w1_codes")
+        w1_sc = held([P, PASSES * H], U8, "w1_sc")
+        nc.vector.tensor_copy(
+            w1_codes[:].bitcast(U16).rearrange("p (a t m) -> p a t m", a=PASSES, t=PACK),
+            w1_raw[:].bitcast(U16).rearrange("p (a m t) -> p a t m", a=PASSES, t=PACK),
+        )
+        nc.vector.tensor_copy(
+            w1_sc[:].rearrange("p (a t m) -> p a t m", a=PASSES, t=PACK),
+            w1_sc_raw[:].rearrange("p (a m t) -> p a t m", a=PASSES, t=PACK),
+        )
+        gather_words(1)
+        wgo_pt = placed([P, PACK * PICK], F32, "wgo_pt", 16)
+        for q in range(QUADS):
+            nc.sync.dma_start(wgo_pt[32 * q : 32 * q + 32, :], wgo.rearrange("(p t) m -> p (t m)", t=PACK))
+
+        def w1_pass(acc, a, t, c):
+            col = a * H + t * P
+            nc.tensor.matmul_mx(
+                out=acc[:],
+                lhsT=w1_codes[:, 2 * col : 2 * (col + P)].bitcast(FP4X4),
+                lhsT_scale=w1_sc[:, col : col + P],
+                rhs=v[a][c].bitcast(FP8X4),
+                rhs_scale=v_sc[:, a * S + c * BANK : a * S + (c + 1) * BANK],
+                start=(a == 0),
+                stop=(a == PASSES - 1),
+            )
+
+        accs = [[bank() for t in range(PACK)] for c in range(HALVES)]
+        for a in range(PASSES):
+            for c in range(HALVES):
+                for t in range(PACK):
+                    w1_pass(accs[c][t], a, t, c)
+
+        th = [held([P, S], F32, f"th{t}") for t in range(PACK)]
+
+        def tanh_out(t, c):
+            nc.scalar.activation(th[t][:, c * BANK : (c + 1) * BANK], accs[c][t][:], ACT.Tanh)
+
+        tanh_out(0, 0)
+        tanh_out(1, 0)
+        tanh_out(0, 1)
+        tanh_out(1, 1)
+        for t in range(2, PACK):
+            for c in range(HALVES):
+                tanh_out(t, c)
+
+        def weave_weight(copy, raw, name, kib):
+            woven = placed([P, H * PACK], BF16, name, kib)
+            copy(
+                woven[:].rearrange("p (t m j) -> p m t j", t=PACK, j=PACK),
+                raw[:].rearrange("p (j m t) -> p m t j", j=PACK, t=PACK),
+            )
+            return woven
+
+        def quantize(woven, name):
+            codes = held([P, H], U32, name)
+            scales = held([P, H], U8, name + "_sc")
+            nc.vector.quantize_mx(out=codes[:].bitcast(FP8X4), scales=scales[:], in_=woven[:])
+            return codes, scales
+
+        gain_skip = held([P, PACK], F32, "gain_skip")
+        nc.vector.tensor_tensor(gain_skip[:], gain_pt[:], skip_pt[:], ALU.mult)
+
+        turns = []
+
+        def phase(t):
+            turns.append(placed([P, S], F32, f"turns{t}", (12, 44, 60, 64)[t]))
+            for c in range(HALVES):
+                acc = bank()
+                for a in range(PASSES):
+                    codes, scales = w3_q[a]
+                    nc.tensor.matmul_mx(
+                        out=acc[:],
+                        lhsT=codes[:, t * P : (t + 1) * P].bitcast(FP8X4),
+                        lhsT_scale=scales[:, t * P : (t + 1) * P],
+                        rhs=v[a][c].bitcast(FP8X4),
+                        rhs_scale=v_sc[:, a * S + c * BANK : a * S + (c + 1) * BANK],
+                        start=(a == 0),
+                        stop=(a == PASSES - 1),
+                    )
+                nc.scalar.activation(
+                    turns[t][:, c * BANK : (c + 1) * BANK], acc[:], ACT.Abs, scale=1.0 / (2.0 * math.pi)
+                )
+
+        def add_turned(first, second):
+            acc = bank()
+            for n, src in enumerate((first, second)):
+                for b in range(BLOCKS):
+                    cols = slice(b * P, (b + 1) * P)
+                    nc.tensor.matmul(
+                        acc[:, cols],
+                        lhsT=src[:, cols],
+                        rhs=ident[:],
+                        is_transpose=True,
+                        start=(n == 0 and b == 0),
+                        stop=(n == 1 and b == BLOCKS - 1),
+                    )
+            return acc
+
+        def pick_turns(t):
+            turns_pick = placed([P, PICK], F32, f"turns_pick{t}", (94, 54, 108, 114)[t])
+            nc.vector.tensor_copy(turns_pick[:], turns[t][:].indirect(pick[:]))
+            return turns_pick
+
+        def reduce_turns(t, turns_pick):
+            whole = placed([P, PICK], U32, f"whole{t}", (62, 90, 74, 78)[t])
+            nc.scalar.activation(whole[:], turns_pick[:], ACT.Copy, bias=0.25)
+            shift = placed([P, PICK], F32, f"shift{t}", (66, 100, 102, 104)[t])
+            nc.scalar.activation(shift[:], whole[:], ACT.Copy, bias=0.25, scale=-1.0)
+            return add_turned(shift, turns_pick)
+
+        def cosine(t, frac):
+            cos_t = placed([P, PICK], F32, f"cos_t{t}", (74, 78, 84, 86)[t])
+            nc.scalar.activation(cos_t[:], frac[:], ACT.Sin, scale=2.0 * math.pi)
+            return cos_t
+
+        def second_stage(t):
+            acc = bank()
+            for b in range(BLOCKS):
+                nc.tensor.matmul_mx(
+                    out=acc[:, b * P : (b + 1) * P],
+                    lhsT=x_codes[:, b * P : (b + 1) * P].bitcast(FP8X4),
+                    lhsT_scale=x_sc[:, b * P : (b + 1) * P],
+                    rhs=w2_codes[:, t * P : (t + 1) * P].bitcast(FP8X4),
+                    rhs_scale=w2_sc[:, t * P : (t + 1) * P],
+                    start=True,
+                    stop=True,
+                )
+            tanh_t = placed([P, PICK], F32, f"tanh_t{t}", (70, 82, 88, 92)[t])
+            nc.scalar.activation(tanh_t[:], acc[:], ACT.Tanh)
+            return tanh_t
+
+        out_pt = out.rearrange("(p t) j -> p t j", t=PACK)
+
+        def fill_page(t):
+            page = placed([P, S], F32, f"page{t}", (8, 56, 106, 112)[t])
+            if t < 2:
+                nc.vector.tensor_scalar_mul(page[:], th[t][:], gain_skip[:, t : t + 1])
+            else:
+                nc.scalar.activation(page[:], th[t][:], ACT.Copy, scale=gain_skip[:, t : t + 1])
+            return page
+
+        def worked_over(y_acc):
+            y = ring.tile([P, PICK], F32, name="y")
+            nc.scalar.copy(y[:], y_acc[:])
+            return y
+
+        def put(t, page, y):
+            nc.vector.tensor_tensor(
+                page[:].indirect(pick[:]), y[:], wgo_pt[:, t * PICK : (t + 1) * PICK], ALU.mult
+            )
+            nc.sync.dma_start(out_pt[:, t, :], page[:])
+
+        th_pick = []
+
+        def pick_tanh(t):
+            th_pick.append(placed([P, PICK], F32, f"th_pick{t}", (36, 0, 28, 30)[t]))
+            nc.vector.tensor_copy(th_pick[t][:], th[t][:].indirect(pick[:]))
+
+        def round_h(t):
+            nc.scalar.activation(h_pick[:, t, :], th_pick[t][:], ACT.Copy, scale=gain_pt[:, t : t + 1])
+
+        w3_woven0 = weave_weight(nc.vector.tensor_copy, w3_raw[0], "w3_woven0", 24)
+        pick_tanh(0)
+        w3_q = [quantize(w3_woven0, "w3_q0")]
+        w3_woven1 = weave_weight(nc.vector.tensor_copy, w3_raw[1], "w3_woven1", 28)
+        pick_tanh(1)
+        w3_q.append(quantize(w3_woven1, "w3_q1"))
+        pick_tanh(2)
+        pick_tanh(3)
+        w2_woven = weave_weight(nc.scalar.copy, w2_raw, "w2_woven", 44)
+        h_pick = placed([P, PACK, PICK], BF16, "h_pick", 8)
+        round_h(0)
+        round_h(1)
+        phase(0)
+        round_h(2)
+        round_h(3)
+        picks = [pick_turns(0)]
+        x_woven = placed([P, PICK * PACK], BF16, "x_woven", 54)
+        nc.vector.tensor_copy(
+            x_woven[:].rearrange("p (c i t) -> p c t i", i=4, t=PACK),
+            h_pick[:].rearrange("p t (c i) -> p c t i", i=4),
+        )
+        pages = [fill_page(0)]
+        phase(1)
+        fracs = [reduce_turns(0, picks[0])]
+        w2_codes, w2_sc = quantize(w2_woven, "w2_q")
+        x_codes, x_sc = quantize(x_woven, "x_q")
+        picks.append(pick_turns(1))
+        phase(2)
+        picks.append(pick_turns(2))
+        pages.append(fill_page(1))
+        for t in range(PACK):
+            cos_t = cosine(t, fracs[t])
+            if t == 0:
+                phase(3)
+                picks.append(pick_turns(3))
+            tanh_t = second_stage(t)
+            y_acc = add_turned(tanh_t, cos_t)
+            if t < 2:
+                fracs.append(reduce_turns(t + 1, picks[t + 1]))
+            else:
+                pages.append(fill_page(t))
+            y = worked_over(y_acc)
+            put(t, pages[t], y)
+            if t == 1:
+                fracs.append(reduce_turns(3, picks[3]))

@@ -33,9 +33,9 @@ def tile_list_echo_frame_rework_kernel(
     nc = tc.nc
     with ExitStack() as ctx:
         keep = ctx.enter_context(tc.tile_pool(name="keep", bufs=1))
-        ring = ctx.enter_context(tc.tile_pool(name="ring", bufs=2))
         reuse = ctx.enter_context(tc.tile_pool(name="reuse", bufs=1))
-        psum = ctx.enter_context(tc.psum_pool(name="psum", bufs=8))
+        psum = ctx.enter_context(tc.psum_pool(name="psum", bufs=1))
+        banks = []
 
         def held(shape, dtype, name):
             return keep.tile(shape, dtype, name=name, align_bytes=64)
@@ -44,7 +44,8 @@ def tile_list_echo_frame_rework_kernel(
             return reuse.tile(shape, dtype, name=name, align_bytes=64, offset=kib * 1024)
 
         def bank():
-            return psum.tile([P, BANK], F32, name="bank")
+            banks.append(psum.tile([P, BANK], F32, name=f"bank{len(banks) % 8}"))
+            return banks[-1]
 
         idx = keep.tile([P, S // 16], U16, name="idx")
         pick = keep.tile([P, PICK // 16], U16, name="pick")
@@ -57,6 +58,9 @@ def tile_list_echo_frame_rework_kernel(
         skip_pt = held([P, PACK], F32, "skip_pt")
         ident = held([P, P], F32, "ident")
 
+        warm = held([P, 2], F32, "warm")
+        nc.gpsimd.memset(warm[:, 0:1], 0.0)
+        nc.scalar.activation(warm[:, 1:2], warm[:, 0:1], ACT.Silu)
         nc.gpsimd.memset(w1_sc_raw[:].bitcast(I32), 0)
         nc.vector.memset(tab_sc[32:64, :].bitcast(I32), 0)
         nc.vector.memset(tab_sc[64:128, :].bitcast(I32), 0)
@@ -257,8 +261,8 @@ def tile_list_echo_frame_rework_kernel(
                 nc.scalar.activation(page[:], th[t][:], ACT.Copy, scale=gain_skip[:, t : t + 1])
             return page
 
-        def worked_over(y_acc):
-            y = ring.tile([P, PICK], F32, name="y")
+        def worked_over(t, y_acc):
+            y = placed([P, PICK], F32, f"y{t}", (63, 116, 118, 120)[t])
             nc.scalar.copy(y[:], y_acc[:])
             return y
 
@@ -318,7 +322,7 @@ def tile_list_echo_frame_rework_kernel(
                 fracs.append(reduce_turns(t + 1, picks[t + 1]))
             else:
                 pages.append(fill_page(t))
-            y = worked_over(y_acc)
+            y = worked_over(t, y_acc)
             put(t, pages[t], y)
             if t == 1:
                 fracs.append(reduce_turns(3, picks[3]))

@@ -32,95 +32,85 @@ def tile_list_echo_frame_rework_kernel(
 ):
     nc = tc.nc
     with ExitStack() as ctx:
-        keep = ctx.enter_context(tc.tile_pool(name="keep", bufs=1))
-        reuse = ctx.enter_context(tc.tile_pool(name="reuse", bufs=1))
+        lists = ctx.enter_context(tc.tile_pool(name="lists", bufs=1))
+        sbuf = ctx.enter_context(tc.tile_pool(name="sbuf", bufs=1))
         psum = ctx.enter_context(tc.psum_pool(name="psum", bufs=1))
-        banks = []
+        starts = {"free": 0}
 
-        def held(shape, dtype, name):
-            return keep.tile(shape, dtype, name=name, align_bytes=64)
+        def tile(name, cols, dtype, over=None, half=0):
+            size = cols * (1 if dtype == U8 else 2 if dtype == BF16 else 4)
+            if over is None:
+                starts[name] = starts["free"]
+                starts["free"] = starts[name] + -(-size // 64) * 64
+            else:
+                starts[name] = starts[over] + half * size
+            return sbuf.tile([P, cols], dtype, name=name, align_bytes=64, offset=starts[name])
 
-        def placed(shape, dtype, name, kib):
-            return reuse.tile(shape, dtype, name=name, align_bytes=64, offset=kib * 1024)
+        def bank(n):
+            return psum.tile([P, BANK], F32, name=f"bank{n}")
 
-        def bank():
-            banks.append(psum.tile([P, BANK], F32, name=f"bank{len(banks) % 8}"))
-            return banks[-1]
+        idx = lists.tile([P, S // 16], U16, name="idx")
+        pick = lists.tile([P, PICK // 16], U16, name="pick")
+        tab = [tile(f"tab{a}", T, U32) for a in range(PASSES)]
+        tab_sc = tile("tab_sc", T, U8)
+        w1_raw = tile("w1_raw", PASSES * 2 * H, U8)
+        w1_sc_raw = tile("w1_sc_raw", PASSES * H, U8)
+        v_sc = tile("v_sc", PASSES * S, U8)
+        gain_pt = tile("gain_pt", PACK, F32)
+        skip_pt = tile("skip_pt", PACK, F32)
 
-        idx = keep.tile([P, S // 16], U16, name="idx")
-        pick = keep.tile([P, PICK // 16], U16, name="pick")
-        tab = [placed([P, T], U32, f"tab{a}", 16 * a) for a in range(PASSES)]
-        tab_sc = held([P, T], U8, "tab_sc")
-        w1_raw = held([P, PASSES * 2 * H], U8, "w1_raw")
-        w1_sc_raw = held([P, PASSES * H], U8, "w1_sc_raw")
-        v_sc = held([P, PASSES * S], U8, "v_sc")
-        gain_pt = held([P, PACK], F32, "gain_pt")
-        skip_pt = held([P, PACK], F32, "skip_pt")
-        ident = held([P, P], F32, "ident")
-
-        warm = held([P, 2], F32, "warm")
+        nc.gpsimd.memset(w1_sc_raw[:].bitcast(I32), 0)
+        warm = tile("warm", 2, F32)
         nc.gpsimd.memset(warm[:, 0:1], 0.0)
         nc.scalar.activation(warm[:, 1:2], warm[:, 0:1], ACT.Silu)
-        nc.gpsimd.memset(w1_sc_raw[:].bitcast(I32), 0)
         nc.vector.memset(tab_sc[32:64, :].bitcast(I32), 0)
-        nc.vector.memset(tab_sc[64:128, :].bitcast(I32), 0)
-        nc.vector.memset(v_sc[:].bitcast(I32), 0)
+        nc.gpsimd.memset(tab_sc[64:128, :].bitcast(I32), 0)
+        nc.gpsimd.memset(v_sc[:].bitcast(I32), 0)
 
         def load_table(a):
             words = tab_words[a].rearrange("p t i -> p (t i)")
             nc.sync.dma_start(tab[a][:].bitcast(I32), words.bitcast(I32))
 
+        def load_rows(dst, rows):
+            nc.sync.dma_start(dst[:], rows.rearrange("(p j) n -> p (j n)", j=PACK))
+
+        nc.sync.dma_start(tab_sc[0:32, :].bitcast(I32), tab_scales.rearrange("a q t -> q a t").bitcast(I32))
         nc.sync.dma_start(idx[:], offs)
-        nc.sync.dma_start(tab_sc[0:32, :].bitcast(I32), tab_scales.rearrange("a q t -> (a q) t").bitcast(I32))
-        load_table(0)
-        load_table(1)
-        nc.scalar.dma_start(
+        nc.sync.dma_start(
             w1_raw[:].bitcast(I32).rearrange("p (a c) -> p a c", a=PASSES),
             w1_words.bitcast(I32).rearrange("a p c -> p a c"),
         )
         for q in range(QUADS):
-            nc.gpsimd.dma_start(
+            nc.sync.dma_start(
                 w1_sc_raw[32 * q : 32 * q + 4, :].bitcast(I32).rearrange("r (a c) -> r a c", a=PASSES),
                 w1_scales[:, 4 * q : 4 * q + 4, :].bitcast(I32).rearrange("a r c -> r a c"),
             )
-        nc.gpsimd.dma_start(gain_pt[:], gain.rearrange("(p t) -> p t", t=PACK))
-        nc.gpsimd.dma_start(skip_pt[:], skip.rearrange("(p t) -> p t", t=PACK))
+        load_table(0)
         nc.sync.dma_start(pick[:], pos1)
-        make_identity(nc, ident[:])
 
-        v_sc_rows = held([P, S], U8, "v_sc_rows")
+        v_sc_rows = tile("v_sc_rows", S, U8)
         nc.vector.tensor_copy(v_sc_rows[:], tab_sc[:].indirect(idx[:]))
-        for a in range(PASSES):
-            for q in range(QUADS):
-                row = 16 * a + 4 * q
-                nc.scalar.dma_start(
-                    v_sc[32 * q : 32 * q + 4, a * S : (a + 1) * S].bitcast(I32),
-                    v_sc_rows[row : row + 4, :].bitcast(I32),
-                )
+        ident = tile("ident", P, F32, "tab_sc")
+        make_identity(nc, ident[:])
+        for q in range(QUADS):
+            nc.sync.dma_start(
+                v_sc[32 * q : 32 * q + 4, :].bitcast(I32).rearrange("r (a c) -> r a c", a=PASSES),
+                v_sc_rows[8 * q : 8 * q + 8, :].bitcast(I32),
+            )
+        load_table(1)
+        w3_raw = [tile(f"w3_raw{a}", PACK * H, F32) for a in range(PASSES)]
+        w2_raw = tile("w2_raw", PACK * H, F32)
+        load_rows(w3_raw[0], w3[0 : P * PACK, :])
+        load_rows(w3_raw[1], w3[P * PACK :, :])
+        load_rows(w2_raw, w2)
+        nc.sync.dma_start(gain_pt[:], gain.rearrange("(p t) -> p t", t=PACK))
+        nc.sync.dma_start(skip_pt[:], skip.rearrange("(p t) -> p t", t=PACK))
+        wgo_pt = tile("wgo_pt", PACK * PICK, F32)
+        for q in range(QUADS):
+            nc.sync.dma_start(wgo_pt[32 * q : 32 * q + 32, :], wgo.rearrange("(p t) m -> p (t m)", t=PACK))
 
-        def load_rows(dst, rows):
-            nc.sync.dma_start(dst, rows.rearrange("(p j) n -> p (j n)", j=PACK))
-
-        w3_first = placed([P, PACK * H], F32, "w3_first", 36)
-        load_rows(w3_first[:], w3[0 : P * PACK, :])
-
-        v0 = placed([P, S], U32, "v0", 32)
-        v1 = held([P, S], U32, "v1")
-        v = [[tile[:, c * BANK : (c + 1) * BANK] for c in range(HALVES)] for tile in (v0, v1)]
-
-        def gather_words(a):
-            for c in range(HALVES):
-                offsets = idx[:, c * BANK // 16 : (c + 1) * BANK // 16]
-                nc.vector.tensor_copy(v[a][c], tab[a][:].indirect(offsets))
-
-        gather_words(0)
-        w3_raw = [w3_first, placed([P, PACK * H], F32, "w3_second", 0)]
-        w2_raw = placed([P, PACK * H], F32, "w2_raw", 8)
-        load_rows(w3_raw[1][:], w3[P * PACK :, :])
-        load_rows(w2_raw[:], w2)
-
-        w1_codes = held([P, PASSES * 2 * H], U8, "w1_codes")
-        w1_sc = held([P, PASSES * H], U8, "w1_sc")
+        w1_codes = tile("w1_codes", PASSES * 2 * H, U8)
+        w1_sc = tile("w1_sc", PASSES * H, U8)
         nc.vector.tensor_copy(
             w1_codes[:].bitcast(U16).rearrange("p (a t m) -> p a t m", a=PASSES, t=PACK),
             w1_raw[:].bitcast(U16).rearrange("p (a m t) -> p a t m", a=PASSES, t=PACK),
@@ -129,82 +119,72 @@ def tile_list_echo_frame_rework_kernel(
             w1_sc[:].rearrange("p (a t m) -> p a t m", a=PASSES, t=PACK),
             w1_sc_raw[:].rearrange("p (a m t) -> p a t m", a=PASSES, t=PACK),
         )
-        gather_words(1)
-        wgo_pt = placed([P, PACK * PICK], F32, "wgo_pt", 16)
-        for q in range(QUADS):
-            nc.sync.dma_start(wgo_pt[32 * q : 32 * q + 32, :], wgo.rearrange("(p t) m -> p (t m)", t=PACK))
 
-        def w1_pass(acc, a, t, c):
-            col = a * H + t * P
+        v_words = [tile(f"v{a}", S, U32) for a in range(PASSES)]
+        v = [[words[:, c * BANK : (c + 1) * BANK] for c in range(HALVES)] for words in v_words]
+        for a in range(PASSES):
+            for c in range(HALVES):
+                offsets = idx[:, c * BANK // 16 : (c + 1) * BANK // 16]
+                nc.vector.tensor_copy(v[a][c], tab[a][:].indirect(offsets))
+
+        def table_pass(acc, codes, scales, a, c):
             nc.tensor.matmul_mx(
                 out=acc[:],
-                lhsT=w1_codes[:, 2 * col : 2 * (col + P)].bitcast(FP4X4),
-                lhsT_scale=w1_sc[:, col : col + P],
+                lhsT=codes,
+                lhsT_scale=scales,
                 rhs=v[a][c].bitcast(FP8X4),
                 rhs_scale=v_sc[:, a * S + c * BANK : a * S + (c + 1) * BANK],
                 start=(a == 0),
                 stop=(a == PASSES - 1),
             )
 
-        accs = [[bank() for t in range(PACK)] for c in range(HALVES)]
+        turn = [(t, c) for pair in range(0, PACK, 2) for c in range(HALVES) for t in (pair, pair + 1)]
+        accs = {part: bank(n) for n, part in enumerate(turn)}
         for a in range(PASSES):
             for c in range(HALVES):
                 for t in range(PACK):
-                    w1_pass(accs[c][t], a, t, c)
+                    col = a * H + t * P
+                    codes = w1_codes[:, 2 * col : 2 * (col + P)].bitcast(FP4X4)
+                    table_pass(accs[t, c], codes, w1_sc[:, col : col + P], a, c)
 
-        th = [held([P, S], F32, f"th{t}") for t in range(PACK)]
+        th = [tile(f"th{t}", S, F32) for t in range(PACK)]
+        for t, c in turn:
+            nc.scalar.activation(th[t][:, c * BANK : (c + 1) * BANK], accs[t, c][:], ACT.Tanh)
 
-        def tanh_out(t, c):
-            nc.scalar.activation(th[t][:, c * BANK : (c + 1) * BANK], accs[c][t][:], ACT.Tanh)
-
-        tanh_out(0, 0)
-        tanh_out(1, 0)
-        tanh_out(0, 1)
-        tanh_out(1, 1)
-        for t in range(2, PACK):
-            for c in range(HALVES):
-                tanh_out(t, c)
-
-        def weave_weight(copy, raw, name, kib):
-            woven = placed([P, H * PACK], BF16, name, kib)
+        def weave_weight(copy, raw, name, over=None):
+            woven = tile(name, H * PACK, BF16, over)
             copy(
                 woven[:].rearrange("p (t m j) -> p m t j", t=PACK, j=PACK),
                 raw[:].rearrange("p (j m t) -> p m t j", j=PACK, t=PACK),
             )
             return woven
 
-        def quantize(woven, name):
-            codes = held([P, H], U32, name)
-            scales = held([P, H], U8, name + "_sc")
+        def quantize(woven, name, over=None):
+            codes = tile(name, H, U32, over)
+            scales = tile(name + "_sc", H, U8)
             nc.vector.quantize_mx(out=codes[:].bitcast(FP8X4), scales=scales[:], in_=woven[:])
             return codes, scales
 
-        gain_skip = held([P, PACK], F32, "gain_skip")
-        nc.vector.tensor_tensor(gain_skip[:], gain_pt[:], skip_pt[:], ALU.mult)
-
-        turns = []
+        phase_accs = {}
+        turns = {}
 
         def phase(t):
-            turns.append(placed([P, S], F32, f"turns{t}", (12, 44, 60, 64)[t]))
             for c in range(HALVES):
-                acc = bank()
+                phase_accs[t, c] = bank(HALVES * t + c)
                 for a in range(PASSES):
                     codes, scales = w3_q[a]
-                    nc.tensor.matmul_mx(
-                        out=acc[:],
-                        lhsT=codes[:, t * P : (t + 1) * P].bitcast(FP8X4),
-                        lhsT_scale=scales[:, t * P : (t + 1) * P],
-                        rhs=v[a][c].bitcast(FP8X4),
-                        rhs_scale=v_sc[:, a * S + c * BANK : a * S + (c + 1) * BANK],
-                        start=(a == 0),
-                        stop=(a == PASSES - 1),
-                    )
-                nc.scalar.activation(
-                    turns[t][:, c * BANK : (c + 1) * BANK], acc[:], ACT.Abs, scale=1.0 / (2.0 * math.pi)
-                )
+                    cols = slice(t * P, (t + 1) * P)
+                    table_pass(phase_accs[t, c], codes[:, cols].bitcast(FP8X4), scales[:, cols], a, c)
 
-        def add_turned(first, second):
-            acc = bank()
+        def phase_out(t, c, over=None):
+            if c == 0:
+                turns[t] = tile(f"turns{t}", S, F32, over)
+            nc.scalar.activation(
+                turns[t][:, c * BANK : (c + 1) * BANK], phase_accs[t, c][:], ACT.Abs, scale=1.0 / (2.0 * math.pi)
+            )
+
+        def add_turned(first, second, n_bank):
+            acc = bank(n_bank)
             for n, src in enumerate((first, second)):
                 for b in range(BLOCKS):
                     cols = slice(b * P, (b + 1) * P)
@@ -218,25 +198,28 @@ def tile_list_echo_frame_rework_kernel(
                     )
             return acc
 
-        def pick_turns(t):
-            turns_pick = placed([P, PICK], F32, f"turns_pick{t}", (94, 54, 108, 114)[t])
-            nc.vector.tensor_copy(turns_pick[:], turns[t][:].indirect(pick[:]))
-            return turns_pick
+        def gather(window, name, over=None, half=0):
+            picked = tile(name, PICK, F32, over, half)
+            nc.vector.tensor_copy(picked[:], window[:].indirect(pick[:]))
+            return picked
 
-        def reduce_turns(t, turns_pick):
-            whole = placed([P, PICK], U32, f"whole{t}", (62, 90, 74, 78)[t])
-            nc.scalar.activation(whole[:], turns_pick[:], ACT.Copy, bias=0.25)
-            shift = placed([P, PICK], F32, f"shift{t}", (66, 100, 102, 104)[t])
+        def whole_turns(t, over=None):
+            whole = tile(f"whole{t}", PICK, U32, over)
+            nc.scalar.activation(whole[:], turns_pick[t][:], ACT.Copy, bias=0.25)
+            return whole
+
+        def fraction(t, whole, n_bank, over=None):
+            shift = tile(f"shift{t}", PICK, F32, over)
             nc.scalar.activation(shift[:], whole[:], ACT.Copy, bias=0.25, scale=-1.0)
-            return add_turned(shift, turns_pick)
+            return add_turned(turns_pick[t], shift, n_bank)
 
-        def cosine(t, frac):
-            cos_t = placed([P, PICK], F32, f"cos_t{t}", (74, 78, 84, 86)[t])
+        def cosine(t, frac, over=None):
+            cos_t = tile(f"cos_t{t}", PICK, F32, over)
             nc.scalar.activation(cos_t[:], frac[:], ACT.Sin, scale=2.0 * math.pi)
             return cos_t
 
-        def second_stage(t):
-            acc = bank()
+        def second_stage(t, n_bank, over=None):
+            acc = bank(n_bank)
             for b in range(BLOCKS):
                 nc.tensor.matmul_mx(
                     out=acc[:, b * P : (b + 1) * P],
@@ -247,22 +230,22 @@ def tile_list_echo_frame_rework_kernel(
                     start=True,
                     stop=True,
                 )
-            tanh_t = placed([P, PICK], F32, f"tanh_t{t}", (70, 82, 88, 92)[t])
+            tanh_t = tile(f"tanh_t{t}", PICK, F32, over)
             nc.scalar.activation(tanh_t[:], acc[:], ACT.Tanh)
             return tanh_t
 
         out_pt = out.rearrange("(p t) j -> p t j", t=PACK)
 
-        def fill_page(t):
-            page = placed([P, S], F32, f"page{t}", (8, 56, 106, 112)[t])
-            if t < 2:
+        def fill_page(t, engine, over=None):
+            page = tile(f"page{t}", S, F32, over)
+            if engine == "vector":
                 nc.vector.tensor_scalar_mul(page[:], th[t][:], gain_skip[:, t : t + 1])
             else:
                 nc.scalar.activation(page[:], th[t][:], ACT.Copy, scale=gain_skip[:, t : t + 1])
             return page
 
-        def worked_over(t, y_acc):
-            y = placed([P, PICK], F32, f"y{t}", (63, 116, 118, 120)[t])
+        def worked_over(t, y_acc, over=None):
+            y = tile(f"y{t}", PICK, F32, over)
             nc.scalar.copy(y[:], y_acc[:])
             return y
 
@@ -272,57 +255,75 @@ def tile_list_echo_frame_rework_kernel(
             )
             nc.sync.dma_start(out_pt[:, t, :], page[:])
 
-        th_pick = []
-
-        def pick_tanh(t):
-            th_pick.append(placed([P, PICK], F32, f"th_pick{t}", (36, 0, 28, 30)[t]))
-            nc.vector.tensor_copy(th_pick[t][:], th[t][:].indirect(pick[:]))
-
         def round_h(t):
-            nc.scalar.activation(h_pick[:, t, :], th_pick[t][:], ACT.Copy, scale=gain_pt[:, t : t + 1])
+            nc.scalar.activation(
+                h_pick[:, t * PICK : (t + 1) * PICK], th_pick[t][:], ACT.Copy, scale=gain_pt[:, t : t + 1]
+            )
 
-        w3_woven0 = weave_weight(nc.vector.tensor_copy, w3_raw[0], "w3_woven0", 24)
-        pick_tanh(0)
-        w3_q = [quantize(w3_woven0, "w3_q0")]
-        w3_woven1 = weave_weight(nc.vector.tensor_copy, w3_raw[1], "w3_woven1", 28)
-        pick_tanh(1)
-        w3_q.append(quantize(w3_woven1, "w3_q1"))
-        pick_tanh(2)
-        pick_tanh(3)
-        w2_woven = weave_weight(nc.scalar.copy, w2_raw, "w2_woven", 44)
-        h_pick = placed([P, PACK, PICK], BF16, "h_pick", 8)
-        round_h(0)
-        round_h(1)
-        phase(0)
-        round_h(2)
-        round_h(3)
-        picks = [pick_turns(0)]
-        x_woven = placed([P, PICK * PACK], BF16, "x_woven", 54)
+        w3_woven = [weave_weight(nc.vector.tensor_copy, w3_raw[0], "w3_woven0")]
+        w3_q = [quantize(w3_woven[0], "w3_q0")]
+        w3_woven.append(weave_weight(nc.vector.tensor_copy, w3_raw[1], "w3_woven1"))
+        w3_q.append(quantize(w3_woven[1], "w3_q1"))
+        th_pick = [gather(th[0], "th_pick0", "w3_raw1")]
+        th_pick.append(gather(th[1], "th_pick1", "w3_raw1", 1))
+        th_pick.append(gather(th[2], "th_pick2", "w3_woven1"))
+        th_pick.append(gather(th[3], "th_pick3", "w3_woven1", 1))
+        w2_woven = weave_weight(nc.scalar.copy, w2_raw, "w2_woven")
+        for t in range(PACK):
+            phase(t)
+        phase_out(0, 0)
+        phase_out(0, 1)
+        h_pick = tile("h_pick", PACK * PICK, BF16, "w2_raw")
+        for t in range(PACK):
+            round_h(t)
+        turns_pick = [gather(turns[0], "turns_pick0")]
+        w2_codes, w2_sc = quantize(w2_woven, "w2_q", "th_pick1")
+        x_woven = tile("x_woven", PICK * PACK, BF16)
         nc.vector.tensor_copy(
             x_woven[:].rearrange("p (c i t) -> p c t i", i=4, t=PACK),
-            h_pick[:].rearrange("p t (c i) -> p c t i", i=4),
+            h_pick[:].rearrange("p (t c i) -> p c t i", i=4, t=PACK),
         )
-        pages = [fill_page(0)]
-        phase(1)
-        fracs = [reduce_turns(0, picks[0])]
-        w2_codes, w2_sc = quantize(w2_woven, "w2_q")
+        whole = whole_turns(0)
+        phase_out(1, 0)
+        frac = fraction(0, whole, 0)
+        phase_out(1, 1)
+        gain_skip = tile("gain_skip", PACK, F32)
+        nc.vector.tensor_tensor(gain_skip[:], gain_pt[:], skip_pt[:], ALU.mult)
+        pages = [fill_page(0, "vector", "w3_woven1")]
         x_codes, x_sc = quantize(x_woven, "x_q")
-        picks.append(pick_turns(1))
-        phase(2)
-        picks.append(pick_turns(2))
-        pages.append(fill_page(1))
-        for t in range(PACK):
-            cos_t = cosine(t, fracs[t])
-            if t == 0:
-                phase(3)
-                picks.append(pick_turns(3))
-            tanh_t = second_stage(t)
-            y_acc = add_turned(tanh_t, cos_t)
-            if t < 2:
-                fracs.append(reduce_turns(t + 1, picks[t + 1]))
-            else:
-                pages.append(fill_page(t))
-            y = worked_over(t, y_acc)
-            put(t, pages[t], y)
-            if t == 1:
-                fracs.append(reduce_turns(3, picks[3]))
+        turns_pick.append(gather(turns[1], "turns_pick1", "w2_woven"))
+        phase_out(2, 0)
+        pages.append(fill_page(1, "vector", "x_woven"))
+        cos_t = cosine(0, frac)
+        phase_out(2, 1)
+        turns_pick.append(gather(turns[2], "turns_pick2"))
+        pages.append(fill_page(2, "vector", "turns1"))
+        pages.append(fill_page(3, "vector", "turns2"))
+        tanh_t = second_stage(0, 1)
+        y_acc = add_turned(cos_t, tanh_t, 2)
+        whole = whole_turns(1)
+        phase_out(3, 0)
+        y = worked_over(0, y_acc)
+        put(0, pages[0], y)
+        frac = fraction(1, whole, 1)
+        phase_out(3, 1)
+        turns_pick.append(gather(turns[3], "turns_pick3"))
+        tanh_t = second_stage(1, 3)
+        cos_t = cosine(1, frac)
+        y_acc = add_turned(tanh_t, cos_t, 0)
+        whole = whole_turns(2)
+        tanh_t = second_stage(2, 4)
+        y = worked_over(1, y_acc)
+        put(1, pages[1], y)
+        frac = fraction(2, whole, 3)
+        cos_t = cosine(2, frac)
+        y_acc = add_turned(tanh_t, cos_t, 2)
+        tanh_t = second_stage(3, 5)
+        whole = whole_turns(3, "shift2")
+        y = worked_over(2, y_acc)
+        put(2, pages[2], y)
+        frac = fraction(3, whole, 3)
+        cos_t = cosine(3, frac)
+        y_acc = add_turned(tanh_t, cos_t, 0)
+        y = worked_over(3, y_acc)
+        put(3, pages[3], y)

@@ -127,15 +127,15 @@ def tile_list_echo_frame_rework_kernel(
                 offsets = idx[:, c * BANK // 16 : (c + 1) * BANK // 16]
                 nc.vector.tensor_copy(v[a][c], tab[a][:].indirect(offsets))
 
-        def table_pass(acc, codes, scales, a, c):
+        def table_pass(acc, codes, scales, a, c, order=(0, 1)):
             nc.tensor.matmul_mx(
                 out=acc[:],
                 lhsT=codes,
                 lhsT_scale=scales,
                 rhs=v[a][c].bitcast(FP8X4),
                 rhs_scale=v_sc[:, a * S + c * BANK : a * S + (c + 1) * BANK],
-                start=(a == 0),
-                stop=(a == PASSES - 1),
+                start=(a == order[0]),
+                stop=(a == order[-1]),
             )
 
         turn = [(t, c) for pair in range(0, PACK, 2) for c in range(HALVES) for t in (pair, pair + 1)]
@@ -169,12 +169,13 @@ def tile_list_echo_frame_rework_kernel(
         turns = {}
 
         def phase(t):
+            order = (0, 1) if t == 0 else (1, 0)
             for c in range(HALVES):
                 phase_accs[t, c] = bank(HALVES * t + c)
-                for a in range(PASSES):
+                for a in order:
                     codes, scales = w3_q[a]
                     cols = slice(t * P, (t + 1) * P)
-                    table_pass(phase_accs[t, c], codes[:, cols].bitcast(FP8X4), scales[:, cols], a, c)
+                    table_pass(phase_accs[t, c], codes[:, cols].bitcast(FP8X4), scales[:, cols], a, c, order)
 
         def phase_out(t, c, over=None):
             if c == 0:
@@ -238,7 +239,9 @@ def tile_list_echo_frame_rework_kernel(
 
         def fill_page(t, engine, over=None):
             page = tile(f"page{t}", S, F32, over)
-            if engine == "vector":
+            if engine == "gpsimd":
+                nc.gpsimd.tensor_scalar(page[:], th[t][:], gain_skip[:, t : t + 1], 0.0, ALU.mult, ALU.add)
+            elif engine == "vector":
                 nc.vector.tensor_scalar_mul(page[:], th[t][:], gain_skip[:, t : t + 1])
             else:
                 nc.scalar.activation(page[:], th[t][:], ACT.Copy, scale=gain_skip[:, t : t + 1])
@@ -260,70 +263,55 @@ def tile_list_echo_frame_rework_kernel(
                 h_pick[:, t * PICK : (t + 1) * PICK], th_pick[t][:], ACT.Copy, scale=gain_pt[:, t : t + 1]
             )
 
+        def gpsimd_copy(dst, src):
+            nc.gpsimd.tensor_scalar(dst, src, 1.0, 0.0, ALU.mult, ALU.add)
+
         w3_woven = [weave_weight(nc.vector.tensor_copy, w3_raw[0], "w3_woven0")]
         w3_q = [quantize(w3_woven[0], "w3_q0")]
         w3_woven.append(weave_weight(nc.vector.tensor_copy, w3_raw[1], "w3_woven1"))
         w3_q.append(quantize(w3_woven[1], "w3_q1"))
-        th_pick = [gather(th[0], "th_pick0", "w3_raw1")]
-        th_pick.append(gather(th[1], "th_pick1", "w3_raw1", 1))
-        th_pick.append(gather(th[2], "th_pick2", "w3_woven1"))
-        th_pick.append(gather(th[3], "th_pick3", "w3_woven1", 1))
-        w2_woven = weave_weight(nc.scalar.copy, w2_raw, "w2_woven")
+        th_pick = [gather(th[t], f"th_pick{t}", "w3_raw1", t) for t in range(PACK)]
+        w2_woven = weave_weight(gpsimd_copy, w2_raw, "w2_woven", "w3_woven1")
+        gain_skip = tile("gain_skip", PACK, F32, "w2_raw")
+        nc.gpsimd.tensor_tensor(gain_skip[:], gain_pt[:], skip_pt[:], ALU.mult)
         for t in range(PACK):
             phase(t)
+        h_pick = tile("h_pick", PACK * PICK, BF16)
         phase_out(0, 0)
         phase_out(0, 1)
-        h_pick = tile("h_pick", PACK * PICK, BF16, "w2_raw")
-        for t in range(PACK):
-            round_h(t)
         turns_pick = [gather(turns[0], "turns_pick0")]
-        w2_codes, w2_sc = quantize(w2_woven, "w2_q", "th_pick1")
+        round_h(0)
+        round_h(1)
+        phase_out(1, 0)
+        round_h(2)
+        phase_out(1, 1)
+        round_h(3)
         x_woven = tile("x_woven", PICK * PACK, BF16)
         nc.vector.tensor_copy(
             x_woven[:].rearrange("p (c i t) -> p c t i", i=4, t=PACK),
             h_pick[:].rearrange("p (t c i) -> p c t i", i=4, t=PACK),
         )
-        whole = whole_turns(0)
-        phase_out(1, 0)
-        frac = fraction(0, whole, 0)
-        phase_out(1, 1)
-        gain_skip = tile("gain_skip", PACK, F32)
-        nc.vector.tensor_tensor(gain_skip[:], gain_pt[:], skip_pt[:], ALU.mult)
-        pages = [fill_page(0, "vector", "w3_woven1")]
+        w2_codes, w2_sc = quantize(w2_woven, "w2_q", "th_pick3")
         x_codes, x_sc = quantize(x_woven, "x_q")
-        turns_pick.append(gather(turns[1], "turns_pick1", "w2_woven"))
+        pages = {0: fill_page(0, "gpsimd", "w2_woven"), 2: fill_page(2, "gpsimd", "x_woven")}
         phase_out(2, 0)
-        pages.append(fill_page(1, "vector", "x_woven"))
-        cos_t = cosine(0, frac)
+        whole = whole_turns(0)
         phase_out(2, 1)
-        turns_pick.append(gather(turns[2], "turns_pick2"))
-        pages.append(fill_page(2, "vector", "turns1"))
-        pages.append(fill_page(3, "vector", "turns2"))
-        tanh_t = second_stage(0, 1)
-        y_acc = add_turned(cos_t, tanh_t, 2)
-        whole = whole_turns(1)
+        frac = fraction(0, whole, 0)
         phase_out(3, 0)
-        y = worked_over(0, y_acc)
-        put(0, pages[0], y)
-        frac = fraction(1, whole, 1)
         phase_out(3, 1)
+        turns_pick.append(gather(turns[1], "turns_pick1", "h_pick"))
+        turns_pick.append(gather(turns[2], "turns_pick2", "h_pick", 1))
         turns_pick.append(gather(turns[3], "turns_pick3"))
-        tanh_t = second_stage(1, 3)
-        cos_t = cosine(1, frac)
-        y_acc = add_turned(tanh_t, cos_t, 0)
-        whole = whole_turns(2)
-        tanh_t = second_stage(2, 4)
-        y = worked_over(1, y_acc)
-        put(1, pages[1], y)
-        frac = fraction(2, whole, 3)
-        cos_t = cosine(2, frac)
-        y_acc = add_turned(tanh_t, cos_t, 2)
-        tanh_t = second_stage(3, 5)
-        whole = whole_turns(3, "shift2")
-        y = worked_over(2, y_acc)
-        put(2, pages[2], y)
-        frac = fraction(3, whole, 3)
-        cos_t = cosine(3, frac)
-        y_acc = add_turned(tanh_t, cos_t, 0)
-        y = worked_over(3, y_acc)
-        put(3, pages[3], y)
+        pages[1] = fill_page(1, "vector", "turns3")
+        for t in range(PACK):
+            if t > 0:
+                whole = whole_turns(t, ("shift0", "tanh_t0", "cos_t1")[t - 1])
+                frac = fraction(t, whole, (1, 2, 0)[t - 1])
+            cos_t = cosine(t, frac, (None, None, "w3_raw0", None)[t])
+            tanh_t = second_stage(t, (1, 3, 6, 7)[t], (None, None, "shift1", "shift2")[t])
+            operands = (cos_t, tanh_t) if t == 0 else (tanh_t, cos_t)
+            y = worked_over(t, add_turned(*operands, (2, 0, 4, 5)[t]))
+            if t == PACK - 1:
+                pages[t] = fill_page(t, "scalar", "cos_t2")
+            put(t, pages[t], y)

import math
from contextlib import ExitStack

import concourse.mybir as mybir
from concourse.masks import make_identity

K, T, S, PICK, H = 1024, 4096, 1024, 512, 512
FLOPS = 2 * K * H * S * 2 + 2 * H * H * PICK

F32 = mybir.dt.float32
BF16 = mybir.dt.bfloat16
I32 = mybir.dt.int32
U32 = mybir.dt.uint32
U16 = mybir.dt.uint16
U8 = mybir.dt.uint8
FP8X4 = mybir.dt.float8_e4m3fn_x4
FP4X4 = mybir.dt.float4_e2m1fn_x4
ACT = mybir.ActivationFunctionType
ALU = mybir.AluOpType

P = 128
PACK = 4
PASSES = K // (P * PACK)
BANK = 512
HALVES = S // BANK
QUADS = 4
BLOCKS = PICK // P


def tile_list_echo_frame_rework_kernel(
    tc, tab_words, tab_scales, offs, w1_words, w1_scales, gain, pos1, w2, w3, skip, wgo, out
):
    nc = tc.nc
    with ExitStack() as ctx:
        lists = ctx.enter_context(tc.tile_pool(name="lists", bufs=1))
        sbuf = ctx.enter_context(tc.tile_pool(name="sbuf", bufs=1))
        psum = ctx.enter_context(tc.psum_pool(name="psum", bufs=1))
        starts = {"free": 0}

        def tile(name, cols, dtype, over=None, half=0):
            size = cols * (1 if dtype == U8 else 2 if dtype == BF16 else 4)
            if over is None:
                starts[name] = starts["free"]
                starts["free"] = starts[name] + -(-size // 64) * 64
            else:
                starts[name] = starts[over] + half * size
            return sbuf.tile([P, cols], dtype, name=name, align_bytes=64, offset=starts[name])

        def bank(n):
            return psum.tile([P, BANK], F32, name=f"bank{n}")

        idx = lists.tile([P, S // 16], U16, name="idx")
        pick = lists.tile([P, PICK // 16], U16, name="pick")
        tab = [tile(f"tab{a}", T, U32) for a in range(PASSES)]
        tab_sc = tile("tab_sc", T, U8)
        w1_raw = tile("w1_raw", PASSES * 2 * H, U8)
        w1_sc_raw = tile("w1_sc_raw", PASSES * H, U8)
        v_sc = tile("v_sc", PASSES * S, U8)
        gain_pt = tile("gain_pt", PACK, F32)
        skip_pt = tile("skip_pt", PACK, F32)

        nc.gpsimd.memset(w1_sc_raw[:].bitcast(I32), 0)
        warm = tile("warm", 2, F32)
        nc.gpsimd.memset(warm[:, 0:1], 0.0)
        nc.scalar.activation(warm[:, 1:2], warm[:, 0:1], ACT.Silu)
        nc.vector.memset(tab_sc[32:64, :].bitcast(I32), 0)
        nc.gpsimd.memset(tab_sc[64:128, :].bitcast(I32), 0)
        nc.gpsimd.memset(v_sc[:].bitcast(I32), 0)

        def load_table(a):
            words = tab_words[a].rearrange("p t i -> p (t i)")
            nc.sync.dma_start(tab[a][:].bitcast(I32), words.bitcast(I32))

        def load_rows(dst, rows):
            nc.sync.dma_start(dst[:], rows.rearrange("(p j) n -> p (j n)", j=PACK))

        nc.sync.dma_start(tab_sc[0:32, :].bitcast(I32), tab_scales.rearrange("a q t -> q a t").bitcast(I32))
        nc.sync.dma_start(idx[:], offs)
        nc.sync.dma_start(
            w1_raw[:].bitcast(I32).rearrange("p (a c) -> p a c", a=PASSES),
            w1_words.bitcast(I32).rearrange("a p c -> p a c"),
        )
        for q in range(QUADS):
            nc.sync.dma_start(
                w1_sc_raw[32 * q : 32 * q + 4, :].bitcast(I32).rearrange("r (a c) -> r a c", a=PASSES),
                w1_scales[:, 4 * q : 4 * q + 4, :].bitcast(I32).rearrange("a r c -> r a c"),
            )
        load_table(0)
        nc.sync.dma_start(pick[:], pos1)

        v_sc_rows = tile("v_sc_rows", S, U8)
        nc.vector.tensor_copy(v_sc_rows[:], tab_sc[:].indirect(idx[:]))
        ident = tile("ident", P, F32, "tab_sc")
        make_identity(nc, ident[:])
        for q in range(QUADS):
            nc.sync.dma_start(
                v_sc[32 * q : 32 * q + 4, :].bitcast(I32).rearrange("r (a c) -> r a c", a=PASSES),
                v_sc_rows[8 * q : 8 * q + 8, :].bitcast(I32),
            )
        load_table(1)
        w3_raw = [tile(f"w3_raw{a}", PACK * H, F32) for a in range(PASSES)]
        w2_raw = tile("w2_raw", PACK * H, F32)
        load_rows(w3_raw[0], w3[0 : P * PACK, :])
        load_rows(w3_raw[1], w3[P * PACK :, :])
        load_rows(w2_raw, w2)
        nc.sync.dma_start(gain_pt[:], gain.rearrange("(p t) -> p t", t=PACK))
        nc.sync.dma_start(skip_pt[:], skip.rearrange("(p t) -> p t", t=PACK))
        wgo_pt = tile("wgo_pt", PACK * PICK, F32)
        for q in range(QUADS):
            nc.sync.dma_start(wgo_pt[32 * q : 32 * q + 32, :], wgo.rearrange("(p t) m -> p (t m)", t=PACK))

        w1_codes = tile("w1_codes", PASSES * 2 * H, U8)
        w1_sc = tile("w1_sc", PASSES * H, U8)
        nc.vector.tensor_copy(
            w1_codes[:].bitcast(U16).rearrange("p (a t m) -> p a t m", a=PASSES, t=PACK),
            w1_raw[:].bitcast(U16).rearrange("p (a m t) -> p a t m", a=PASSES, t=PACK),
        )
        nc.vector.tensor_copy(
            w1_sc[:].rearrange("p (a t m) -> p a t m", a=PASSES, t=PACK),
            w1_sc_raw[:].rearrange("p (a m t) -> p a t m", a=PASSES, t=PACK),
        )

        v_words = [tile(f"v{a}", S, U32) for a in range(PASSES)]
        v = [[words[:, c * BANK : (c + 1) * BANK] for c in range(HALVES)] for words in v_words]
        for a in range(PASSES):
            for c in range(HALVES):
                offsets = idx[:, c * BANK // 16 : (c + 1) * BANK // 16]
                nc.vector.tensor_copy(v[a][c], tab[a][:].indirect(offsets))

        def table_pass(acc, codes, scales, a, c, order=(0, 1)):
            nc.tensor.matmul_mx(
                out=acc[:],
                lhsT=codes,
                lhsT_scale=scales,
                rhs=v[a][c].bitcast(FP8X4),
                rhs_scale=v_sc[:, a * S + c * BANK : a * S + (c + 1) * BANK],
                start=(a == order[0]),
                stop=(a == order[-1]),
            )

        turn = [(t, c) for pair in range(0, PACK, 2) for c in range(HALVES) for t in (pair, pair + 1)]
        accs = {part: bank(n) for n, part in enumerate(turn)}
        for a in range(PASSES):
            for c in range(HALVES):
                for t in range(PACK):
                    col = a * H + t * P
                    codes = w1_codes[:, 2 * col : 2 * (col + P)].bitcast(FP4X4)
                    table_pass(accs[t, c], codes, w1_sc[:, col : col + P], a, c)

        th = [tile(f"th{t}", S, F32) for t in range(PACK)]
        for t, c in turn:
            nc.scalar.activation(th[t][:, c * BANK : (c + 1) * BANK], accs[t, c][:], ACT.Tanh)

        def weave_weight(copy, raw, name, over=None):
            woven = tile(name, H * PACK, BF16, over)
            copy(
                woven[:].rearrange("p (t m j) -> p m t j", t=PACK, j=PACK),
                raw[:].rearrange("p (j m t) -> p m t j", j=PACK, t=PACK),
            )
            return woven

        def quantize(woven, name, over=None):
            codes = tile(name, H, U32, over)
            scales = tile(name + "_sc", H, U8)
            nc.vector.quantize_mx(out=codes[:].bitcast(FP8X4), scales=scales[:], in_=woven[:])
            return codes, scales

        phase_accs = {}
        turns = {}

        def phase(t):
            order = (0, 1) if t == 0 else (1, 0)
            for c in range(HALVES):
                phase_accs[t, c] = bank(HALVES * t + c)
                for a in order:
                    codes, scales = w3_q[a]
                    cols = slice(t * P, (t + 1) * P)
                    table_pass(phase_accs[t, c], codes[:, cols].bitcast(FP8X4), scales[:, cols], a, c, order)

        def phase_out(t, c, over=None):
            if c == 0:
                turns[t] = tile(f"turns{t}", S, F32, over)
            nc.scalar.activation(
                turns[t][:, c * BANK : (c + 1) * BANK], phase_accs[t, c][:], ACT.Abs, scale=1.0 / (2.0 * math.pi)
            )

        def add_turned(first, second, n_bank):
            acc = bank(n_bank)
            for n, src in enumerate((first, second)):
                for b in range(BLOCKS):
                    cols = slice(b * P, (b + 1) * P)
                    nc.tensor.matmul(
                        acc[:, cols],
                        lhsT=src[:, cols],
                        rhs=ident[:],
                        is_transpose=True,
                        start=(n == 0 and b == 0),
                        stop=(n == 1 and b == BLOCKS - 1),
                    )
            return acc

        def gather(window, name, over=None, half=0):
            picked = tile(name, PICK, F32, over, half)
            nc.vector.tensor_copy(picked[:], window[:].indirect(pick[:]))
            return picked

        def whole_turns(t, over=None):
            whole = tile(f"whole{t}", PICK, U32, over)
            nc.scalar.activation(whole[:], turns_pick[t][:], ACT.Copy, bias=0.25)
            return whole

        def fraction(t, whole, n_bank, over=None):
            shift = tile(f"shift{t}", PICK, F32, over)
            nc.scalar.activation(shift[:], whole[:], ACT.Copy, bias=0.25, scale=-1.0)
            return add_turned(turns_pick[t], shift, n_bank)

        def cosine(t, frac, over=None):
            cos_t = tile(f"cos_t{t}", PICK, F32, over)
            nc.scalar.activation(cos_t[:], frac[:], ACT.Sin, scale=2.0 * math.pi)
            return cos_t

        def second_stage(t, n_bank, over=None):
            acc = bank(n_bank)
            for b in range(BLOCKS):
                nc.tensor.matmul_mx(
                    out=acc[:, b * P : (b + 1) * P],
                    lhsT=x_codes[:, b * P : (b + 1) * P].bitcast(FP8X4),
                    lhsT_scale=x_sc[:, b * P : (b + 1) * P],
                    rhs=w2_codes[:, t * P : (t + 1) * P].bitcast(FP8X4),
                    rhs_scale=w2_sc[:, t * P : (t + 1) * P],
                    start=True,
                    stop=True,
                )
            tanh_t = tile(f"tanh_t{t}", PICK, F32, over)
            nc.scalar.activation(tanh_t[:], acc[:], ACT.Tanh)
            return tanh_t

        out_pt = out.rearrange("(p t) j -> p t j", t=PACK)

        def fill_page(t, engine, over=None):
            page = tile(f"page{t}", S, F32, over)
            if engine == "gpsimd":
                nc.gpsimd.tensor_scalar(page[:], th[t][:], gain_skip[:, t : t + 1], 0.0, ALU.mult, ALU.add)
            elif engine == "vector":
                nc.vector.tensor_scalar_mul(page[:], th[t][:], gain_skip[:, t : t + 1])
            else:
                nc.scalar.activation(page[:], th[t][:], ACT.Copy, scale=gain_skip[:, t : t + 1])
            return page

        def worked_over(t, y_acc, over=None):
            y = tile(f"y{t}", PICK, F32, over)
            nc.scalar.copy(y[:], y_acc[:])
            return y

        def put(t, page, y):
            nc.vector.tensor_tensor(
                page[:].indirect(pick[:]), y[:], wgo_pt[:, t * PICK : (t + 1) * PICK], ALU.mult
            )
            nc.sync.dma_start(out_pt[:, t, :], page[:])

        def round_h(t):
            nc.scalar.activation(
                h_pick[:, t * PICK : (t + 1) * PICK], th_pick[t][:], ACT.Copy, scale=gain_pt[:, t : t + 1]
            )

        def gpsimd_copy(dst, src):
            nc.gpsimd.tensor_scalar(dst, src, 1.0, 0.0, ALU.mult, ALU.add)

        w3_woven = [weave_weight(nc.vector.tensor_copy, w3_raw[0], "w3_woven0")]
        w3_q = [quantize(w3_woven[0], "w3_q0")]
        w3_woven.append(weave_weight(nc.vector.tensor_copy, w3_raw[1], "w3_woven1"))
        w3_q.append(quantize(w3_woven[1], "w3_q1"))
        th_pick = [gather(th[t], f"th_pick{t}", "w3_raw1", t) for t in range(PACK)]
        w2_woven = weave_weight(gpsimd_copy, w2_raw, "w2_woven", "w3_woven1")
        gain_skip = tile("gain_skip", PACK, F32, "w2_raw")
        nc.gpsimd.tensor_tensor(gain_skip[:], gain_pt[:], skip_pt[:], ALU.mult)
        for t in range(PACK):
            phase(t)
        h_pick = tile("h_pick", PACK * PICK, BF16)
        phase_out(0, 0)
        phase_out(0, 1)
        turns_pick = [gather(turns[0], "turns_pick0")]
        round_h(0)
        round_h(1)
        phase_out(1, 0)
        round_h(2)
        phase_out(1, 1)
        round_h(3)
        x_woven = tile("x_woven", PICK * PACK, BF16)
        nc.vector.tensor_copy(
            x_woven[:].rearrange("p (c i t) -> p c t i", i=4, t=PACK),
            h_pick[:].rearrange("p (t c i) -> p c t i", i=4, t=PACK),
        )
        w2_codes, w2_sc = quantize(w2_woven, "w2_q", "th_pick3")
        x_codes, x_sc = quantize(x_woven, "x_q")
        pages = {0: fill_page(0, "gpsimd", "w2_woven"), 2: fill_page(2, "gpsimd", "x_woven")}
        phase_out(2, 0)
        whole = whole_turns(0)
        phase_out(2, 1)
        frac = fraction(0, whole, 0)
        phase_out(3, 0)
        phase_out(3, 1)
        turns_pick.append(gather(turns[1], "turns_pick1", "h_pick"))
        turns_pick.append(gather(turns[2], "turns_pick2", "h_pick", 1))
        turns_pick.append(gather(turns[3], "turns_pick3"))
        pages[1] = fill_page(1, "vector", "turns3")
        for t in range(PACK):
            if t > 0:
                whole = whole_turns(t, ("shift0", "tanh_t0", "cos_t1")[t - 1])
                frac = fraction(t, whole, (1, 2, 0)[t - 1])
            cos_t = cosine(t, frac, (None, None, "w3_raw0", None)[t])
            tanh_t = second_stage(t, (1, 3, 6, 7)[t], (None, None, "shift1", "shift2")[t])
            operands = (cos_t, tanh_t) if t == 0 else (tanh_t, cos_t)
            y = worked_over(t, add_turned(*operands, (2, 0, 4, 5)[t]))
            if t == PACK - 1:
                pages[t] = fill_page(t, "scalar", "cos_t2")
            put(t, pages[t], y)
